import numpy as np, ml_dtypes
CORES = [1,17,65,89,97,113]
N = 6
KT, C = 1, 128
B = 1
def setup_inputs(rng):
    return {"x": rng.standard_normal((N, 128, KT * C), dtype=np.float32).astype(ml_dtypes.bfloat16)}
def setup_inputs_big(rng):
    d = setup_inputs(rng)
    for k in ("x",): d[k] = (d[k].astype(np.float32) * 1024.0).astype(d[k].dtype)
    return d
def setup_inputs_small(rng):
    d = setup_inputs(rng)
    for k in ("x",): d[k] = (d[k].astype(np.float32) * (1 / 1024.0)).astype(d[k].dtype)
    return d
def setup_inputs_apart(rng):
    d = setup_inputs(rng)
    f = (10.0 ** rng.permutation(np.linspace(-1.5, 1.5, N))).astype(np.float32).reshape(N, 1, 1)
    for k in ("x",): d[k] = (d[k].astype(np.float32) * f).astype(d[k].dtype)
    return d
def reference(x):
    X = x.astype(np.float64)
    y = np.full((N, C, (2 * B + 1) * C), np.nan)
    for r in range(N):
        for i in range(2 * B + 1):
            s = (r + i - B) % N
            if s != r: y[r][:, C * i:C * i + C] = sum(X[r][:, C * t:C * t + C].T @ X[s][:, C * t:C * t + C] for t in range(KT))
    return {"y": y.astype(ml_dtypes.bfloat16 if x.dtype != np.float64 else np.float64)}

from concourse.bass import DstId, RemoteDMATransfer

W = 128

SCRATCH = {
    "xs": ("sbuf", [128, W], "bfloat16"),
    "xd": ("dram", [128, W], "bfloat16"),
    "rel": ("dram", [128, W], "bfloat16"),
    "land0": ("sbuf", [128, W], "bfloat16"),
    "land2": ("sbuf", [128, W], "bfloat16"),
    "ps0": ("psum", [128, 512], "float32"),
    "ps2": ("psum", [128, 512], "float32"),
    "out0": ("sbuf", [128, W], "bfloat16"),
    "out2": ("sbuf", [128, W], "bfloat16"),
}
SEMAPHORES = ["staged", "loaded", "sent", "relin", "arr0", "arr2", "mm0", "mm2", "cp0", "cp2", "st0", "st2"]

TO_RELAY_ENGINES = 4
FORWARD_ENGINES = 8
DIRECT_ENGINES = 8


def pick(mask, n, skip=0):
    bits = [b for b in range(mask.bit_length()) if (mask >> b) & 1]
    m = 0
    for b in bits[skip:skip + n]:
        m |= 1 << b
    return m


def plan(T, topo):
    cores = list(T.cores)
    n = len(cores)
    every = range(topo.CHIPS * topo.CORES_PER_CHIP)
    taken = set(cores)
    routes = []
    for r in range(n):
        for step, blk in ((1, 0), (-1, 2)):
            s = (r + step) % n
            src, dst = cores[r], cores[s]
            relay = None
            if not topo.may_write(src, dst):
                cand = [c for c in every
                        if topo.chip(c) == topo.chip(src) and c not in taken and topo.may_write(c, dst)]
                cand.sort(key=lambda c: (topo.die(c) != topo.die(src), c))
                relay = cand[0]
                taken.add(relay)
            routes.append((r, s, blk, relay))
    return routes


def shares(routes, r):
    via = sum(1 for rt in routes if rt[0] == r and rt[3] is not None)
    direct = sum(1 for rt in routes if rt[0] == r and rt[3] is None)
    return (TO_RELAY_ENGINES // via if via else 0), (DIRECT_ENGINES // direct if direct else 0)


def send(g, topo, core, src, items, n, local_sem):
    if not items:
        return 0
    if len(items) == 1:
        dst, buf, sem = items[0]
        rid, pid, _ = topo.addr(dst)
        g.remote_dma(out_ap=buf[:], in_ap=src[:], remote_sem=sem, local_sem=local_sem, pid=pid, routing_id=rid,
                     dma_engine_mask=pick(topo.mask(core, dst), n))
        return n
    trs = []
    for i, (dst, buf, sem) in enumerate(items):
        rid, pid, _ = topo.addr(dst)
        trs.append(RemoteDMATransfer(dst_ids=[DstId(rid=rid, pnc=pid)], dma_engine_mask=pick(topo.mask(core, dst), n, i * n),
                                     remote_sem=sem, src=src[:], dst=buf[:]))
    g.remote_dma_fused(trs, local_sem=local_sem)
    return n * len(items)


def rank_program(g, core, T, topo):
    routes = plan(T, topo)
    cores = list(T.cores)
    rank = T.rank_of(core)

    if rank is None:
        for r, s, blk, relay in routes:
            if relay == core:
                g.wait_ge(T.sem.relin, shares(routes, r)[0])
                got = send(g, topo, core, T.rel, [(cores[s], T["land%d" % blk], T.sem["arr%d" % blk])],
                           FORWARD_ENGINES, T.sem.sent)
                g.wait_ge(T.sem.sent, got)
        return

    mine = [rt for rt in routes if rt[0] == rank]
    via = [(rt[3], T.rel, T.sem.relin) for rt in mine if rt[3] is not None]
    direct = [(cores[rt[1]], T["land%d" % rt[2]], T.sem["arr%d" % rt[2]]) for rt in mine if rt[3] is None]
    n_via, n_direct = shares(routes, rank)

    if via:
        g.sync.dma_start(T.xd[:], T.x[:]).then_inc(T.sem.staged, 16)
        g.sync.dma_start(T.xs[:], T.x[:]).then_inc(T.sem.loaded, 16)
        g.wait_ge(T.sem.staged, 16)
        src = T.xd
    else:
        g.sync.dma_start(T.xs[:], T.x[:]).then_inc(T.sem.loaded, 16)
        g.wait_ge(T.sem.loaded, 16)
        src = T.xs
    left = send(g, topo, core, src, via, n_via, T.sem.sent)
    left += send(g, topo, core, src, direct, n_direct, T.sem.sent)

    incoming = sorted((rt for rt in routes if rt[1] == rank), key=lambda rt: rt[3] is not None)
    g.tensor.wait_ge(T.sem.loaded, 16)
    for k, (r, s, blk, relay) in enumerate(incoming):
        n_in = FORWARD_ENGINES if relay is not None else shares(routes, r)[1]
        ps, out = T["ps%d" % blk], T["out%d" % blk]
        g.tensor.wait_ge(T.sem["arr%d" % blk], n_in)
        g.tensor.matmul(ps[:, 0:W], T.xs[:], T["land%d" % blk][:], True, True).then_inc(T.sem["mm%d" % blk], 1)
        g.vector.wait_ge(T.sem["mm%d" % blk], 1)
        g.vector.tensor_copy(out[:], ps[:, 0:W]).then_inc(T.sem["cp%d" % blk], 1)
        q = (g.sync, g.scalar)[k % 2]
        q.wait_ge(T.sem["cp%d" % blk], 1)
        q.dma_start(T.y[:, blk * W:(blk + 1) * W], out[:]).then_inc(T.sem["st%d" % blk], 16)
        q.wait_ge(T.sem["st%d" % blk], 16)
    g.wait_ge(T.sem.sent, left)
